import numpy as np
import ml_dtypes


def mxq(x, axis, fmt="e4m3"):
    dtype, down = {"e4m3": (ml_dtypes.float8_e4m3fn, 7), "e5m2": (ml_dtypes.float8_e5m2, 14)}[fmt]
    v = np.moveaxis(np.asarray(x, np.float32).astype(ml_dtypes.bfloat16).astype(np.float64), axis, -1)
    blocks = v.reshape(v.shape[:-1] + (-1, 32))
    amax = np.abs(blocks).max(-1, keepdims=True)
    byte = np.maximum(np.where(amax > 0, np.frexp(amax)[1] - 1 + 127, 0) - down, 1)
    scale = np.exp2(byte - 127.0)
    codes = (blocks / scale).astype(np.float32).astype(dtype).astype(np.float64)
    return np.moveaxis((codes * scale).reshape(v.shape), -1, axis)


WIDE = False


def mx_kscale(k):
    if not WIDE:
        return np.ones(k)
    levels = np.array([10, -10, 5, -5, 0])
    if k % 512:
        return np.exp2(np.random.permutation(np.resize(levels, k // 32))).repeat(32)
    a = np.empty((k // 512, 16))
    for p in range(k // 512):
        a[p, :8] = np.random.permutation(np.resize(levels, 8))
        for g in range(8):
            far = levels[np.abs(levels - a[p, g]) >= 10]
            a[p, g + 8] = far[np.random.randint(len(far))]
    return np.exp2(a.ravel()).repeat(32)


def f64(x):
    return np.asarray(x).astype(np.float64)


def striped(idx):
    return np.tile(idx.reshape(-1, 16).T, (8, 1)).astype(np.uint16)


def unstriped(offs):
    return offs[:16].T.reshape(-1).astype(np.int64)


def pack_weight(w):
    k, n = w.shape
    w = f64(np.asarray(w, np.float32).astype(ml_dtypes.bfloat16)).reshape(k // 32, 32, n)
    amax = np.abs(w).max(1)
    byte = np.clip(np.where(amax > 0, np.frexp(amax)[1] - 1 + 127 - 7, 1), 1, 254)
    scaled = (w * np.exp2(127.0 - byte)[:, None, :]).reshape(k, n).astype(np.float32)
    words = np.ascontiguousarray(scaled.reshape(k // 512, 128, 4, n).transpose(0, 1, 3, 2)).astype(ml_dtypes.float8_e4m3fn).view(np.uint8)
    return words, np.ascontiguousarray(byte.astype(np.uint8).reshape(k // 512, 16, n))


def unpack_weight(words, scales):
    g, p, n, _ = words.shape
    vals = np.ascontiguousarray(words).view(ml_dtypes.float8_e4m3fn).astype(np.float64) * np.repeat(np.exp2(scales.astype(np.float64) - 127.0), 8, axis=1)[..., None]
    return vals.transpose(0, 1, 3, 2).reshape(g * 512, n)


K, T, E, C, N = 512, 2048, 2, 256, 256


def by_expert(wq, xq):
    return np.concatenate([wq[e].T @ xq[:, e * C:(e + 1) * C] for e in range(E)], axis=1)


def setup_inputs():
    n = np.random.standard_normal
    s = mx_kscale(K)[:, None]
    packed = [pack_weight(m) for m in n((E, K, N)) / np.sqrt(K) / s[None]]
    return {
        "xT": (n((K, T)) * s).astype(np.float32),
        "w_words": np.stack([m[0] for m in packed]),
        "w_scales": np.stack([m[1] for m in packed]),
        "gate": np.tile(np.random.uniform(0.2, 1.0, E * C), (N, 1)).astype(np.float32),
        "offs": striped(np.random.permutation(T)[:E * C]),
    }


def reference(xT, w_words, w_scales, gate, offs):
    idx = unstriped(offs)
    xq = mxq(f64(xT)[:, idx], 0, "e4m3")
    w = np.stack([unpack_weight(w_words[e], w_scales[e]) for e in range(E)])
    y = by_expert(w, xq)
    out = np.zeros((N, T))
    out[:, idx] = f64(gate) * y
    return out

@@ -1,0 +1,99 @@
+from contextlib import ExitStack
+
+import concourse.mybir as mybir
+
+K, T, E, C, N = 512, 2048, 2, 256, 256
+SLOTS = E * C
+FLOPS = 2 * K * N * SLOTS
+
+F32 = mybir.dt.float32
+BF16 = mybir.dt.bfloat16
+I32 = mybir.dt.int32
+U32 = mybir.dt.uint32
+U16 = mybir.dt.uint16
+U8 = mybir.dt.uint8
+FP8X4 = mybir.dt.float8_e4m3fn_x4
+MULT = mybir.AluOpType.mult
+
+P = 128
+PACK = 4
+BLOCKS = N // P
+LIST_COLS = C // 16
+
+
+def tile_routed_moe_kernel(tc, xT, w_words, w_scales, gate, offs, out):
+    nc = tc.nc
+    with ExitStack() as ctx:
+        keep = ctx.enter_context(tc.tile_pool(name="keep", bufs=1))
+        psum = ctx.enter_context(tc.psum_pool(name="psum", bufs=1))
+
+        offsets = keep.tile([P, SLOTS // 16], U16, name="offsets")
+        nc.sync.dma_start(offsets[:], offs)
+
+        planes = xT.rearrange("(p t) n -> p t n", t=PACK)
+        raw = [keep.tile([P, T], F32, name="raw%d" % t) for t in range(PACK)]
+        for t in range(PACK):
+            nc.sync.dma_start(raw[t][:], planes[:, t, :])
+
+        w_sc = keep.tile([P, E, N], U8, name="w_sc", align_bytes=64)
+        nc.vector.memset(w_sc[:].rearrange("p e n -> p (e n)").bitcast(I32), 0)
+        for q in range(4):
+            nc.sync.dma_start(
+                w_sc[32 * q : 32 * q + 4, :, :].bitcast(I32),
+                w_scales[:, 0, 4 * q : 4 * q + 4, :].rearrange("e r n -> r e n").bitcast(I32),
+            )
+        w_codes = keep.tile([P, E, N], I32, name="w_codes", align_bytes=64)
+        nc.sync.dma_start(w_codes[:], w_words.rearrange("e a p n r -> p (e a) (n r)").bitcast(I32))
+        gate_sb = keep.tile([P, BLOCKS, SLOTS], F32, name="gate_sb")
+        nc.sync.dma_start(gate_sb[:], gate.rearrange("(b p) j -> p b j", p=P))
+
+        win = [keep.tile([P, T], F32, name="win%d" % b) for b in range(BLOCKS)]
+        for b in range(BLOCKS):
+            nc.vector.memset(win[b][:], 0.0)
+
+        xg = keep.tile([P, SLOTS, PACK], BF16, name="xg", align_bytes=64)
+        x_codes = [keep.tile([P, C], U32, name="x_codes%d" % e, align_bytes=64) for e in range(E)]
+        x_sc = [keep.tile([P, C], U8, name="x_sc%d" % e, align_bytes=64) for e in range(E)]
+        lists = [offsets[:, e * LIST_COLS : (e + 1) * LIST_COLS] for e in range(E)]
+
+        for t in range(PACK - 1):
+            nc.vector.tensor_copy(xg[:, :, t], raw[t][:].indirect(offsets[:]))
+
+        t = PACK - 1
+        OVER = 2
+        nc.vector.tensor_copy(xg[:, 0 : C + 16 * OVER, t], raw[t][:].indirect(offsets[:, 0 : LIST_COLS + OVER]))
+        nc.vector.quantize_mx(
+            out=x_codes[0][:].bitcast(FP8X4),
+            scales=x_sc[0][:],
+            in_=xg[:, 0:C, :].rearrange("p w j -> p (w j)"),
+        )
+        nc.vector.tensor_copy(xg[:, C:SLOTS, t], raw[t][:].indirect(lists[1]))
+        nc.vector.quantize_mx(
+            out=x_codes[1][:].bitcast(FP8X4),
+            scales=x_sc[1][:],
+            in_=xg[:, C:SLOTS, :].rearrange("p w j -> p (w j)"),
+        )
+
+        acc = [[psum.tile([P, C], F32, name="acc%d%d" % (b, e)) for e in range(E)] for b in range(BLOCKS)]
+        for e in range(E):
+            for b in range(BLOCKS):
+                nc.tensor.matmul_mx(
+                    out=acc[b][e][:],
+                    lhsT=w_codes[:, e, b * P : (b + 1) * P].bitcast(FP8X4),
+                    lhsT_scale=w_sc[:, e, b * P : (b + 1) * P],
+                    rhs=x_codes[e][:].bitcast(FP8X4),
+                    rhs_scale=x_sc[e][:],
+                    start=True,
+                    stop=True,
+                )
+
+        y = [keep.tile([P, SLOTS], F32, name="y%d" % b) for b in range(BLOCKS)]
+        for e in range(E):
+            for b in range(BLOCKS):
+                nc.scalar.copy(y[b][:, e * C : (e + 1) * C], acc[b][e][:])
+
+        for b in range(BLOCKS):
+            for e in range(E):
+                cols = slice(e * C, (e + 1) * C)
+                nc.vector.tensor_tensor(out=win[b][:].indirect(lists[e]), in0=y[b][:, cols], in1=gate_sb[:, b, cols], op=MULT)
+            nc.sync.dma_start(out[b * P : (b + 1) * P, :], win[b][:])

@@ -32,16 +32,16 @@ def tile_routed_moe_kernel(tc, xT, w_words, w_scales, gate, offs, out):
 
         planes = xT.rearrange("(p t) n -> p t n", t=PACK)
         raw = [keep.tile([P, T], F32, name="raw%d" % t) for t in range(PACK)]
-        for t in range(PACK):
-            nc.sync.dma_start(raw[t][:], planes[:, t, :])
-
         w_sc = keep.tile([P, E, N], U8, name="w_sc", align_bytes=64)
         nc.vector.memset(w_sc[:].rearrange("p e n -> p (e n)").bitcast(I32), 0)
+        nc.sync.dma_start(raw[0][:], planes[:, 0, :])
         for q in range(4):
             nc.sync.dma_start(
                 w_sc[32 * q : 32 * q + 4, :, :].bitcast(I32),
                 w_scales[:, 0, 4 * q : 4 * q + 4, :].rearrange("e r n -> r e n").bitcast(I32),
             )
+        for t in range(1, PACK):
+            nc.sync.dma_start(raw[t][:], planes[:, t, :])
         w_codes = keep.tile([P, E, N], I32, name="w_codes", align_bytes=64)
         nc.sync.dma_start(w_codes[:], w_words.rearrange("e a p n r -> p (e a) (n r)").bitcast(I32))
         gate_sb = keep.tile([P, BLOCKS, SLOTS], F32, name="gate_sb")

@@ -60,7 +60,7 @@ def tile_routed_moe_kernel(tc, xT, w_words, w_scales, gate, offs, out):
             nc.vector.tensor_copy(xg[:, :, t], raw[t][:].indirect(offsets[:]))
 
         t = PACK - 1
-        OVER = 2
+        OVER = 1
         nc.vector.tensor_copy(xg[:, 0 : C + 16 * OVER, t], raw[t][:].indirect(offsets[:, 0 : LIST_COLS + OVER]))
         nc.vector.quantize_mx(
             out=x_codes[0][:].bitcast(FP8X4),

@@ -74,23 +74,33 @@ def tile_routed_moe_kernel(tc, xT, w_words, w_scales, gate, offs, out):
             in_=xg[:, C:SLOTS, :].rearrange("p w j -> p (w j)"),
         )
 
-        acc = [[psum.tile([P, C], F32, name="acc%d%d" % (b, e)) for e in range(E)] for b in range(BLOCKS)]
-        for e in range(E):
-            for b in range(BLOCKS):
-                nc.tensor.matmul_mx(
-                    out=acc[b][e][:],
-                    lhsT=w_codes[:, e, b * P : (b + 1) * P].bitcast(FP8X4),
-                    lhsT_scale=w_sc[:, e, b * P : (b + 1) * P],
-                    rhs=x_codes[e][:].bitcast(FP8X4),
-                    rhs_scale=x_sc[e][:],
-                    start=True,
-                    stop=True,
-                )
-
         y = [keep.tile([P, SLOTS], F32, name="y%d" % b) for b in range(BLOCKS)]
-        for e in range(E):
-            for b in range(BLOCKS):
-                nc.scalar.copy(y[b][:, e * C : (e + 1) * C], acc[b][e][:])
+        for h in range(2):
+            half = slice(h * P, (h + 1) * P)
+            first = psum.tile([P, P], F32, name="first%d" % h)
+            nc.tensor.matmul_mx(
+                out=first[:],
+                lhsT=w_codes[:, 0, 0:P].bitcast(FP8X4),
+                lhsT_scale=w_sc[:, 0, 0:P],
+                rhs=x_codes[0][:, half].bitcast(FP8X4),
+                rhs_scale=x_sc[0][:, half],
+                start=True,
+                stop=True,
+            )
+            nc.scalar.copy(y[0][:, half], first[:])
+        rest = [(1, 0), (0, 1), (1, 1)]
+        acc = [psum.tile([P, C], F32, name="acc%d%d" % (b, e)) for b, e in rest]
+        for i, (b, e) in enumerate(rest):
+            nc.tensor.matmul_mx(
+                out=acc[i][:],
+                lhsT=w_codes[:, e, b * P : (b + 1) * P].bitcast(FP8X4),
+                lhsT_scale=w_sc[:, e, b * P : (b + 1) * P],
+                rhs=x_codes[e][:].bitcast(FP8X4),
+                rhs_scale=x_sc[e][:],
+                start=True,
+                stop=True,
+            )
+            nc.scalar.copy(y[b][:, e * C : (e + 1) * C], acc[i][:])
 
         for b in range(BLOCKS):
             for e in range(E):

@@ -28,13 +28,13 @@ def tile_routed_moe_kernel(tc, xT, w_words, w_scales, gate, offs, out):
         psum = ctx.enter_context(tc.psum_pool(name="psum", bufs=1))
 
         offsets = keep.tile([P, SLOTS // 16], U16, name="offsets")
-        nc.sync.dma_start(offsets[:], offs)
 
         planes = xT.rearrange("(p t) n -> p t n", t=PACK)
         raw = [keep.tile([P, T], F32, name="raw%d" % t) for t in range(PACK)]
         w_sc = keep.tile([P, E, N], U8, name="w_sc", align_bytes=64)
         nc.vector.memset(w_sc[:].rearrange("p e n -> p (e n)").bitcast(I32), 0)
         nc.sync.dma_start(raw[0][:], planes[:, 0, :])
+        nc.sync.dma_start(offsets[:], offs)
         for q in range(4):
             nc.sync.dma_start(
                 w_sc[32 * q : 32 * q + 4, :, :].bitcast(I32),

from contextlib import ExitStack

import concourse.mybir as mybir

K, T, E, C, N = 512, 2048, 2, 256, 256
SLOTS = E * C
FLOPS = 2 * K * N * SLOTS

F32 = mybir.dt.float32
BF16 = mybir.dt.bfloat16
I32 = mybir.dt.int32
U32 = mybir.dt.uint32
U16 = mybir.dt.uint16
U8 = mybir.dt.uint8
FP8X4 = mybir.dt.float8_e4m3fn_x4
MULT = mybir.AluOpType.mult

P = 128
PACK = 4
BLOCKS = N // P
LIST_COLS = C // 16


def tile_routed_moe_kernel(tc, xT, w_words, w_scales, gate, offs, out):
    nc = tc.nc
    with ExitStack() as ctx:
        keep = ctx.enter_context(tc.tile_pool(name="keep", bufs=1))
        psum = ctx.enter_context(tc.psum_pool(name="psum", bufs=1))

        offsets = keep.tile([P, SLOTS // 16], U16, name="offsets")

        planes = xT.rearrange("(p t) n -> p t n", t=PACK)
        raw = [keep.tile([P, T], F32, name="raw%d" % t) for t in range(PACK)]
        w_sc = keep.tile([P, E, N], U8, name="w_sc", align_bytes=64)
        nc.vector.memset(w_sc[:].rearrange("p e n -> p (e n)").bitcast(I32), 0)
        nc.sync.dma_start(raw[0][:], planes[:, 0, :])
        nc.sync.dma_start(offsets[:], offs)
        for q in range(4):
            nc.sync.dma_start(
                w_sc[32 * q : 32 * q + 4, :, :].bitcast(I32),
                w_scales[:, 0, 4 * q : 4 * q + 4, :].rearrange("e r n -> r e n").bitcast(I32),
            )
        for t in range(1, PACK):
            nc.sync.dma_start(raw[t][:], planes[:, t, :])
        w_codes = keep.tile([P, E, N], I32, name="w_codes", align_bytes=64)
        nc.sync.dma_start(w_codes[:], w_words.rearrange("e a p n r -> p (e a) (n r)").bitcast(I32))
        gate_sb = keep.tile([P, BLOCKS, SLOTS], F32, name="gate_sb")
        nc.sync.dma_start(gate_sb[:], gate.rearrange("(b p) j -> p b j", p=P))

        win = [keep.tile([P, T], F32, name="win%d" % b) for b in range(BLOCKS)]
        for b in range(BLOCKS):
            nc.vector.memset(win[b][:], 0.0)

        xg = keep.tile([P, SLOTS, PACK], BF16, name="xg", align_bytes=64)
        x_codes = [keep.tile([P, C], U32, name="x_codes%d" % e, align_bytes=64) for e in range(E)]
        x_sc = [keep.tile([P, C], U8, name="x_sc%d" % e, align_bytes=64) for e in range(E)]
        lists = [offsets[:, e * LIST_COLS : (e + 1) * LIST_COLS] for e in range(E)]

        for t in range(PACK - 1):
            nc.vector.tensor_copy(xg[:, :, t], raw[t][:].indirect(offsets[:]))

        t = PACK - 1
        OVER = 1
        nc.vector.tensor_copy(xg[:, 0 : C + 16 * OVER, t], raw[t][:].indirect(offsets[:, 0 : LIST_COLS + OVER]))
        nc.vector.quantize_mx(
            out=x_codes[0][:].bitcast(FP8X4),
            scales=x_sc[0][:],
            in_=xg[:, 0:C, :].rearrange("p w j -> p (w j)"),
        )
        nc.vector.tensor_copy(xg[:, C:SLOTS, t], raw[t][:].indirect(lists[1]))
        nc.vector.quantize_mx(
            out=x_codes[1][:].bitcast(FP8X4),
            scales=x_sc[1][:],
            in_=xg[:, C:SLOTS, :].rearrange("p w j -> p (w j)"),
        )

        y = [keep.tile([P, SLOTS], F32, name="y%d" % b) for b in range(BLOCKS)]
        for h in range(2):
            half = slice(h * P, (h + 1) * P)
            first = psum.tile([P, P], F32, name="first%d" % h)
            nc.tensor.matmul_mx(
                out=first[:],
                lhsT=w_codes[:, 0, 0:P].bitcast(FP8X4),
                lhsT_scale=w_sc[:, 0, 0:P],
                rhs=x_codes[0][:, half].bitcast(FP8X4),
                rhs_scale=x_sc[0][:, half],
                start=True,
                stop=True,
            )
            nc.scalar.copy(y[0][:, half], first[:])
        rest = [(1, 0), (0, 1), (1, 1)]
        acc = [psum.tile([P, C], F32, name="acc%d%d" % (b, e)) for b, e in rest]
        for i, (b, e) in enumerate(rest):
            nc.tensor.matmul_mx(
                out=acc[i][:],
                lhsT=w_codes[:, e, b * P : (b + 1) * P].bitcast(FP8X4),
                lhsT_scale=w_sc[:, e, b * P : (b + 1) * P],
                rhs=x_codes[e][:].bitcast(FP8X4),
                rhs_scale=x_sc[e][:],
                start=True,
                stop=True,
            )
            nc.scalar.copy(y[b][:, e * C : (e + 1) * C], acc[i][:])

        for b in range(BLOCKS):
            for e in range(E):
                cols = slice(e * C, (e + 1) * C)
                nc.vector.tensor_tensor(out=win[b][:].indirect(lists[e]), in0=y[b][:, cols], in1=gate_sb[:, b, cols], op=MULT)
            nc.sync.dma_start(out[b * P : (b + 1) * P, :], win[b][:])
